import numpy as np
import ml_dtypes


def mxq(x, axis, fmt="e4m3"):
    dtype, down = {"e4m3": (ml_dtypes.float8_e4m3fn, 7), "e5m2": (ml_dtypes.float8_e5m2, 14)}[fmt]
    v = np.moveaxis(np.asarray(x, np.float32).astype(ml_dtypes.bfloat16).astype(np.float64), axis, -1)
    blocks = v.reshape(v.shape[:-1] + (-1, 32))
    amax = np.abs(blocks).max(-1, keepdims=True)
    byte = np.maximum(np.where(amax > 0, np.frexp(amax)[1] - 1 + 127, 0) - down, 1)
    scale = np.exp2(byte - 127.0)
    codes = (blocks / scale).astype(np.float32).astype(dtype).astype(np.float64)
    return np.moveaxis((codes * scale).reshape(v.shape), -1, axis)


WIDE = False


def mx_kscale(k):
    if not WIDE:
        return np.ones(k)
    levels = np.array([10, -10, 5, -5, 0])
    if k % 512:
        return np.exp2(np.random.permutation(np.resize(levels, k // 32))).repeat(32)
    a = np.empty((k // 512, 16))
    for p in range(k // 512):
        a[p, :8] = np.random.permutation(np.resize(levels, 8))
        for g in range(8):
            far = levels[np.abs(levels - a[p, g]) >= 10]
            a[p, g + 8] = far[np.random.randint(len(far))]
    return np.exp2(a.ravel()).repeat(32)


def f64(x):
    return np.asarray(x).astype(np.float64)


def striped(idx):
    return np.tile(np.asarray(idx).reshape(-1, 16).T, (8, 1)).astype(np.uint16)


def unstriped(offs):
    return offs[:16].T.reshape(-1).astype(np.int64)


def striped8(idx):
    return np.asarray(idx).reshape(8, -1, 16).transpose(0, 2, 1).reshape(128, -1).astype(np.uint16)


def unstriped8(offs):
    return offs.reshape(8, 16, -1).transpose(0, 2, 1).reshape(8, -1).astype(np.int64)


def pick8(x, idx, run):
    r = np.arange(len(x))
    return x[r[:, None], idx[r % (8 * run) // run]]


E2M1 = np.array([0.0, 0.5, 1.0, 1.5, 2.0, 3.0, 4.0, 6.0, -0.0, -0.5, -1.0, -1.5, -2.0, -3.0, -4.0, -6.0])


def pack_weight(w, fmt):
    k, n = w.shape
    w = f64(np.asarray(w, np.float32).astype(ml_dtypes.bfloat16)).reshape(k // 32, 32, n)
    amax = np.abs(w).max(1)
    if fmt == "e4m3":
        byte = np.frexp(amax)[1] - 1 + 127 - 7
    else:
        mant, ex = np.frexp(amax / 6.0)
        byte = np.where(mant > 0.5, ex, ex - 1) + 127
    byte = np.clip(np.where(amax > 0, byte, 1), 1, 254)
    scaled = (w * np.exp2(127.0 - byte)[:, None, :]).reshape(k, n).astype(np.float32)
    by_word = np.ascontiguousarray(scaled.reshape(k // 512, 128, 4, n).transpose(0, 1, 3, 2))
    if fmt == "e4m3":
        words = by_word.astype(ml_dtypes.float8_e4m3fn).view(np.uint8)
    else:
        c = by_word.astype(ml_dtypes.float4_e2m1fn).view(np.uint8) & 0xF
        words = (c[..., 0::2] | (c[..., 1::2] << 4)).reshape(k // 512, 128, 2 * n)
    return np.ascontiguousarray(words), np.ascontiguousarray(byte.astype(np.uint8).reshape(k // 512, 16, n))


def unpack_weight(words, scales, fmt):
    g, _, n = scales.shape
    words = np.ascontiguousarray(words).reshape(g, 128, n, -1)
    if fmt == "e4m3":
        vals = words.view(ml_dtypes.float8_e4m3fn).astype(np.float64)
    else:
        nib = np.empty((g, 128, n, 4), np.uint8)
        nib[..., 0::2] = words & 0xF
        nib[..., 1::2] = words >> 4
        vals = E2M1[nib]
    vals = vals * np.repeat(np.exp2(scales.astype(np.float64) - 127.0), 8, axis=1)[..., None]
    return vals.transpose(0, 1, 3, 2).reshape(g * 512, n)


K, T, J, I, L, N = 1024, 2048, 512, 512, 512, 512


def setup_inputs():
    n = np.random.standard_normal
    idx = np.random.permutation(T)[:J]
    idx2 = np.stack([np.random.randint(0, J, I) for _ in range(8)])
    fk = mx_kscale(K)
    fl = mx_kscale(L)
    xtp = pack_weight(n((K, T)) / fk[:, None], "e4m3")
    xip = pack_weight(n((L, I)) / fl[:, None], "e2m1")
    wip = pack_weight(n((L, N)) * 1 / np.sqrt(L) * fl[:, None], "e4m3")
    return {
        "xt_words": xtp[0],
        "xt_scales": xtp[1],
        "w": (n((K, N)) * 1 / np.sqrt(K) * fk[:, None]).astype(np.float32),
        "xi_words": xip[0],
        "xi_scales": xip[1],
        "wi_words": wip[0],
        "wi_scales": wip[1],
        "offs": striped(idx),
        "offs2": striped8(idx2),
    }


def reference(xt_words, xt_scales, w, xi_words, xi_scales, wi_words, wi_scales, offs, offs2):
    idx = unstriped(offs)
    idx2 = unstriped8(offs2)
    xtu = unpack_weight(xt_words, xt_scales, "e4m3")
    xiu = unpack_weight(xi_words, xi_scales, "e2m1")
    wiu = unpack_weight(wi_words, wi_scales, "e4m3")
    wq = mxq(f64(w), 0, "e4m3")
    xtidxg = xtu[:, idx]
    z = wq.T @ xtidxg
    q = wiu.T @ xiu
    y = pick8(z, idx2, 64) * q
    return y

@@ -1,0 +1,170 @@
+from contextlib import ExitStack
+
+import concourse.mybir as mybir
+
+K, T, J, I, L, N = 1024, 2048, 512, 512, 512, 512
+FLOPS = 2 * K * N * J + 2 * L * N * I
+
+F32 = mybir.dt.float32
+BF16 = mybir.dt.bfloat16
+I32 = mybir.dt.int32
+U32 = mybir.dt.uint32
+U16 = mybir.dt.uint16
+U8 = mybir.dt.uint8
+FP8X4 = mybir.dt.float8_e4m3fn_x4
+FP4X4 = mybir.dt.float4_e2m1fn_x4
+MULT = mybir.AluOpType.mult
+
+P = 128
+PACK = 4
+K_PASS = P * PACK
+PASSES = K // K_PASS
+TILES = N // P
+HALF = J // 2
+VECTOR_TILES = 3
+
+
+def tile_list_shared_list_then_heads_kernel(
+    tc, xt_words, xt_scales, w, xi_words, xi_scales, wi_words, wi_scales, offs, offs2, out
+):
+    nc = tc.nc
+    with ExitStack() as ctx:
+        sb = ctx.enter_context(tc.tile_pool(name="sb", bufs=1))
+        psum = ctx.enter_context(tc.psum_pool(name="psum", bufs=1))
+        psq = ctx.enter_context(tc.psum_pool(name="psq", bufs=3))
+
+        slot_list = sb.tile([P, J // 16], U16, name="slot_list")
+        head_lists = sb.tile([P, I // 16], U16, name="head_lists")
+        xt_tab = [sb.tile([P, T], I32, name=f"xt_tab{a}", align_bytes=64) for a in range(PASSES)]
+        xt_sc_tab = sb.tile([P, T], U8, name="xt_sc_tab", align_bytes=64)
+        w_raw = [sb.tile([P, PACK, N], F32, name=f"w_raw{a}", align_bytes=64) for a in range(PASSES)]
+        wi_raw = sb.tile([P, N], I32, name="wi_raw", align_bytes=64)
+        wi_sc_raw = sb.tile([P, N], U8, name="wi_sc_raw", align_bytes=64)
+        xi_codes = sb.tile([P, 2 * I], U8, name="xi_codes", align_bytes=64)
+        xi_sc = sb.tile([P, I], U8, name="xi_sc", align_bytes=64)
+
+        nc.vector.memset(wi_sc_raw[:].bitcast(I32), 0)
+        nc.vector.memset(xt_sc_tab[:].bitcast(I32), 0)
+
+        def load_w(a):
+            rows = w[a * K_PASS : (a + 1) * K_PASS, :]
+            nc.sync.dma_start(out=w_raw[a][:], in_=rows.rearrange("(p j) n -> p j n", j=PACK))
+
+        def load_xt(a):
+            nc.sync.dma_start(out=xt_tab[a][:], in_=xt_words[a].rearrange("p c r -> p (c r)").bitcast(I32))
+
+        nc.sync.dma_start(slot_list[:], offs)
+        for quad in range(4):
+            nc.gpsimd.dma_start(
+                out=xi_sc[32 * quad : 32 * quad + 4, :].bitcast(I32),
+                in_=xi_scales[0, 4 * quad : 4 * quad + 4, :].bitcast(I32),
+            )
+        load_w(0)
+        nc.sync.dma_start(out=wi_raw[:], in_=wi_words[0].rearrange("p c r -> p (c r)").bitcast(I32))
+        nc.sync.dma_start(out=xi_codes[:].bitcast(I32), in_=xi_words[0].bitcast(I32))
+        for quad in range(4):
+            nc.sync.dma_start(
+                out=wi_sc_raw[32 * quad : 32 * quad + 4, :].bitcast(I32),
+                in_=wi_scales[0, 4 * quad : 4 * quad + 4, :].bitcast(I32),
+            )
+        load_xt(0)
+        for quad in range(4):
+            nc.sync.dma_start(
+                out=xt_sc_tab[32 * quad : 32 * quad + 4 * PASSES, :].bitcast(I32),
+                in_=xt_scales[:, 4 * quad : 4 * quad + 4, :].bitcast(I32),
+            )
+        load_w(1)
+        nc.sync.dma_start(head_lists[:], offs2)
+        load_xt(1)
+
+        wi_codes = sb.tile([P, TILES, P], U32, name="wi_codes", align_bytes=64)
+        wi_sc = sb.tile([P, TILES, P], U8, name="wi_sc", align_bytes=64)
+        xt_sc = sb.tile([P, J], U8, name="xt_sc", align_bytes=64)
+
+        w_codes = [sb.tile([P, N], U32, name=f"w_codes{a}", align_bytes=64) for a in range(PASSES)]
+        w_sc = [sb.tile([P, N], U8, name=f"w_sc{a}", align_bytes=64) for a in range(PASSES)]
+        grouped = [sb.tile([P, TILES, P, PACK], BF16, name=f"grouped{a}", align_bytes=64) for a in range(PASSES)]
+
+        def quantise_w(a):
+            src = w_raw[a][:].rearrange("p j (q m) -> p q j m", m=TILES)
+            dst = grouped[a][:].rearrange("p m q j -> p q j m")
+            nc.vector.tensor_copy(out=dst[:, :, :, :VECTOR_TILES], in_=src[:, :, :, :VECTOR_TILES])
+            nc.scalar.copy(out=dst[:, :, :, VECTOR_TILES:], in_=src[:, :, :, VECTOR_TILES:])
+            nc.vector.quantize_mx(
+                out=w_codes[a][:].bitcast(FP8X4),
+                scales=w_sc[a][:],
+                in_=grouped[a][:].rearrange("p m q j -> p (m q j)"),
+            )
+
+        xt_codes = [sb.tile([P, J], U32, name=f"xt_codes{a}", align_bytes=64) for a in range(PASSES)]
+
+        def gather_xt(a, lo, hi):
+            nc.vector.tensor_copy(
+                xt_codes[a][:, lo:hi], xt_tab[a][:].bitcast(U32).indirect(slot_list[:, lo // 16 : hi // 16])
+            )
+
+        def z_pass(acc, a, m, lo, hi):
+            cols = slice(m * P, (m + 1) * P)
+            nc.tensor.matmul_mx(
+                out=acc,
+                lhsT=w_codes[a][:, cols].bitcast(FP8X4),
+                lhsT_scale=w_sc[a][:, cols],
+                rhs=xt_codes[a][:, lo:hi].bitcast(FP8X4),
+                rhs_scale=xt_sc[4 * a :, lo:hi],
+                start=(a == 0),
+                stop=(a == PASSES - 1),
+            )
+
+        quantise_w(0)
+        nc.vector.tensor_copy(
+            out=wi_codes[:].rearrange("p m q -> p q m"),
+            in_=wi_raw[:].bitcast(U32).rearrange("p (q m) -> p q m", m=TILES),
+        )
+        nc.vector.tensor_copy(
+            out=wi_sc[:].rearrange("p m q -> p q m"),
+            in_=wi_sc_raw[:].rearrange("p (q m) -> p q m", m=TILES),
+        )
+        gather_xt(0, 0, J)
+        nc.vector.tensor_copy(xt_sc[:], xt_sc_tab[:].indirect(slot_list[:]))
+
+        q = [sb.tile([P, I], F32, name=f"q{m}", align_bytes=64) for m in range(TILES)]
+        for m in range(TILES):
+            q_acc = psq.tile([P, I], F32, name="q_acc")
+            nc.tensor.matmul_mx(
+                out=q_acc[:],
+                lhsT=wi_codes[:, m, :].bitcast(FP8X4),
+                lhsT_scale=wi_sc[:, m, :],
+                rhs=xi_codes[:].bitcast(FP4X4),
+                rhs_scale=xi_sc[:],
+                start=True,
+                stop=True,
+            )
+            nc.scalar.copy(out=q[m][:], in_=q_acc[:])
+
+        pieces = [(0, 0, HALF), (0, HALF, J)] + [(m, 0, J) for m in range(1, TILES)]
+        z_acc = [psum.tile([P, hi - lo], F32, name=f"z_acc{m}_{lo}") for m, lo, hi in pieces]
+        for acc, (m, lo, hi) in zip(z_acc, pieces):
+            z_pass(acc[:], 0, m, lo, hi)
+
+        quantise_w(1)
+        gather_xt(1, 0, HALF)
+        gather_xt(1, HALF, J)
+
+        z = [sb.tile([P, J], F32, name=f"z{m}", align_bytes=64) for m in range(TILES)]
+        for acc, (m, lo, hi) in zip(z_acc, pieces):
+            z_pass(acc[:], 1, m, lo, hi)
+            nc.scalar.copy(out=z[m][:, lo:hi], in_=acc[:])
+
+        out_rows = out.rearrange("(p m) i -> p m i", m=TILES)
+        for m in range(TILES):
+            y = sb.tile([P, I], F32, name=f"y{m}", align_bytes=64)
+            last = m == TILES - 1
+            cut = 384 if last else I // 2
+            for lo, hi in ((0, cut), (cut, I)):
+                nc.vector.tensor_tensor(
+                    y[:, lo:hi], z[m][:].indirect(head_lists[:, lo // 16 : hi // 16]), q[m][:, lo:hi], MULT
+                )
+                if last:
+                    nc.sync.dma_start(out=out_rows[:, m, lo:hi], in_=y[:, lo:hi])
+            if not last:
+                nc.sync.dma_start(out=out_rows[:, m, :], in_=y[:])

@@ -22,6 +22,7 @@ PASSES = K // K_PASS
 TILES = N // P
 HALF = J // 2
 VECTOR_TILES = 3
+RUN = 4
 
 
 def tile_list_shared_list_then_heads_kernel(
@@ -38,13 +39,13 @@ def tile_list_shared_list_then_heads_kernel(
         xt_tab = [sb.tile([P, T], I32, name=f"xt_tab{a}", align_bytes=64) for a in range(PASSES)]
         xt_sc_tab = sb.tile([P, T], U8, name="xt_sc_tab", align_bytes=64)
         w_raw = [sb.tile([P, PACK, N], F32, name=f"w_raw{a}", align_bytes=64) for a in range(PASSES)]
-        wi_raw = sb.tile([P, N], I32, name="wi_raw", align_bytes=64)
+        wi_raw = sb.tile([P, N], I32, name="wi_raw", tag="wi_then_xt_sc", align_bytes=64)
         wi_sc_raw = sb.tile([P, N], U8, name="wi_sc_raw", align_bytes=64)
         xi_codes = sb.tile([P, 2 * I], U8, name="xi_codes", align_bytes=64)
         xi_sc = sb.tile([P, I], U8, name="xi_sc", align_bytes=64)
 
-        nc.vector.memset(wi_sc_raw[:].bitcast(I32), 0)
         nc.vector.memset(xt_sc_tab[:].bitcast(I32), 0)
+        nc.vector.memset(wi_sc_raw[:].bitcast(I32), 0)
 
         def load_w(a):
             rows = w[a * K_PASS : (a + 1) * K_PASS, :]
@@ -53,43 +54,42 @@ def tile_list_shared_list_then_heads_kernel(
         def load_xt(a):
             nc.sync.dma_start(out=xt_tab[a][:], in_=xt_words[a].rearrange("p c r -> p (c r)").bitcast(I32))
 
+        load_w(0)
         nc.sync.dma_start(slot_list[:], offs)
         for quad in range(4):
             nc.gpsimd.dma_start(
+                out=xt_sc_tab[32 * quad : 32 * quad + 4 * PASSES, :].bitcast(I32),
+                in_=xt_scales[:, 4 * quad : 4 * quad + 4, :].bitcast(I32),
+            )
+        for quad in range(4):
+            nc.sync.dma_start(
                 out=xi_sc[32 * quad : 32 * quad + 4, :].bitcast(I32),
                 in_=xi_scales[0, 4 * quad : 4 * quad + 4, :].bitcast(I32),
             )
-        load_w(0)
-        nc.sync.dma_start(out=wi_raw[:], in_=wi_words[0].rearrange("p c r -> p (c r)").bitcast(I32))
-        nc.sync.dma_start(out=xi_codes[:].bitcast(I32), in_=xi_words[0].bitcast(I32))
+        nc.sync.dma_start(head_lists[:], offs2)
+        load_xt(0)
         for quad in range(4):
             nc.sync.dma_start(
                 out=wi_sc_raw[32 * quad : 32 * quad + 4, :].bitcast(I32),
                 in_=wi_scales[0, 4 * quad : 4 * quad + 4, :].bitcast(I32),
             )
-        load_xt(0)
-        for quad in range(4):
-            nc.sync.dma_start(
-                out=xt_sc_tab[32 * quad : 32 * quad + 4 * PASSES, :].bitcast(I32),
-                in_=xt_scales[:, 4 * quad : 4 * quad + 4, :].bitcast(I32),
-            )
+        nc.sync.dma_start(out=wi_raw[:], in_=wi_words[0].rearrange("p c r -> p (c r)").bitcast(I32))
+        nc.sync.dma_start(out=xi_codes[:].bitcast(I32), in_=xi_words[0].bitcast(I32))
         load_w(1)
-        nc.sync.dma_start(head_lists[:], offs2)
         load_xt(1)
 
         wi_codes = sb.tile([P, TILES, P], U32, name="wi_codes", align_bytes=64)
         wi_sc = sb.tile([P, TILES, P], U8, name="wi_sc", align_bytes=64)
-        xt_sc = sb.tile([P, J], U8, name="xt_sc", align_bytes=64)
 
         w_codes = [sb.tile([P, N], U32, name=f"w_codes{a}", align_bytes=64) for a in range(PASSES)]
         w_sc = [sb.tile([P, N], U8, name=f"w_sc{a}", align_bytes=64) for a in range(PASSES)]
         grouped = [sb.tile([P, TILES, P, PACK], BF16, name=f"grouped{a}", align_bytes=64) for a in range(PASSES)]
 
         def quantise_w(a):
-            src = w_raw[a][:].rearrange("p j (q m) -> p q j m", m=TILES)
-            dst = grouped[a][:].rearrange("p m q j -> p q j m")
-            nc.vector.tensor_copy(out=dst[:, :, :, :VECTOR_TILES], in_=src[:, :, :, :VECTOR_TILES])
-            nc.scalar.copy(out=dst[:, :, :, VECTOR_TILES:], in_=src[:, :, :, VECTOR_TILES:])
+            src = w_raw[a][:].rearrange("p j (s m u) -> p s m j u", m=TILES, u=RUN)
+            dst = grouped[a][:].rearrange("p m (s u) j -> p s m j u", u=RUN)
+            nc.vector.tensor_copy(out=dst[:, :, :VECTOR_TILES], in_=src[:, :, :VECTOR_TILES])
+            nc.scalar.copy(out=dst[:, :, VECTOR_TILES:], in_=src[:, :, VECTOR_TILES:])
             nc.vector.quantize_mx(
                 out=w_codes[a][:].bitcast(FP8X4),
                 scales=w_sc[a][:],
@@ -116,15 +116,16 @@ def tile_list_shared_list_then_heads_kernel(
             )
 
         quantise_w(0)
-        nc.vector.tensor_copy(
-            out=wi_codes[:].rearrange("p m q -> p q m"),
-            in_=wi_raw[:].bitcast(U32).rearrange("p (q m) -> p q m", m=TILES),
-        )
-        nc.vector.tensor_copy(
-            out=wi_sc[:].rearrange("p m q -> p q m"),
-            in_=wi_sc_raw[:].rearrange("p (q m) -> p q m", m=TILES),
-        )
         gather_xt(0, 0, J)
+        nc.vector.tensor_copy(
+            out=wi_codes[:].rearrange("p m (s u) -> p m s u", u=RUN),
+            in_=wi_raw[:].bitcast(U32).rearrange("p (s m u) -> p m s u", m=TILES, u=RUN),
+        )
+        nc.vector.tensor_copy(
+            out=wi_sc[:].bitcast(I32).rearrange("p m s -> p s m"),
+            in_=wi_sc_raw[:].bitcast(I32).rearrange("p (s m) -> p s m", m=TILES),
+        )
+        xt_sc = sb.tile([P, J], U8, name="xt_sc", tag="wi_then_xt_sc", align_bytes=64)
         nc.vector.tensor_copy(xt_sc[:], xt_sc_tab[:].indirect(slot_list[:]))
 
         q = [sb.tile([P, I], F32, name=f"q{m}", align_bytes=64) for m in range(TILES)]
@@ -155,7 +156,7 @@ def tile_list_shared_list_then_heads_kernel(
             z_pass(acc[:], 1, m, lo, hi)
             nc.scalar.copy(out=z[m][:, lo:hi], in_=acc[:])
 
-        out_rows = out.rearrange("(p m) i -> p m i", m=TILES)
+        out_rows = out.rearrange("(s m u) i -> m s u i", m=TILES, u=RUN)
         for m in range(TILES):
             y = sb.tile([P, I], F32, name=f"y{m}", align_bytes=64)
             last = m == TILES - 1
@@ -165,6 +166,6 @@ def tile_list_shared_list_then_heads_kernel(
                     y[:, lo:hi], z[m][:].indirect(head_lists[:, lo // 16 : hi // 16]), q[m][:, lo:hi], MULT
                 )
                 if last:
-                    nc.sync.dma_start(out=out_rows[:, m, lo:hi], in_=y[:, lo:hi])
+                    nc.sync.dma_start(out=out_rows[m, :, :, lo:hi], in_=y[:, lo:hi])
             if not last:
-                nc.sync.dma_start(out=out_rows[:, m, :], in_=y[:])
+                nc.sync.dma_start(out=out_rows[m], in_=y[:])

@@ -23,6 +23,7 @@ TILES = N // P
 HALF = J // 2
 VECTOR_TILES = 3
 RUN = 4
+XT_PLANE = (8, 12)
 
 
 def tile_list_shared_list_then_heads_kernel(
@@ -32,54 +33,63 @@ def tile_list_shared_list_then_heads_kernel(
     with ExitStack() as ctx:
         sb = ctx.enter_context(tc.tile_pool(name="sb", bufs=1))
         psum = ctx.enter_context(tc.psum_pool(name="psum", bufs=1))
-        psq = ctx.enter_context(tc.psum_pool(name="psq", bufs=3))
+        psq = ctx.enter_context(tc.psum_pool(name="psq", bufs=2))
 
         slot_list = sb.tile([P, J // 16], U16, name="slot_list")
         head_lists = sb.tile([P, I // 16], U16, name="head_lists")
         xt_tab = [sb.tile([P, T], I32, name=f"xt_tab{a}", align_bytes=64) for a in range(PASSES)]
         xt_sc_tab = sb.tile([P, T], U8, name="xt_sc_tab", align_bytes=64)
         w_raw = [sb.tile([P, PACK, N], F32, name=f"w_raw{a}", align_bytes=64) for a in range(PASSES)]
-        wi_raw = sb.tile([P, N], I32, name="wi_raw", tag="wi_then_xt_sc", align_bytes=64)
+        wi_raw = sb.tile([P, N], I32, name="wi_raw", align_bytes=64)
         wi_sc_raw = sb.tile([P, N], U8, name="wi_sc_raw", align_bytes=64)
         xi_codes = sb.tile([P, 2 * I], U8, name="xi_codes", align_bytes=64)
         xi_sc = sb.tile([P, I], U8, name="xi_sc", align_bytes=64)
 
-        nc.vector.memset(xt_sc_tab[:].bitcast(I32), 0)
         nc.vector.memset(wi_sc_raw[:].bitcast(I32), 0)
+        nc.vector.memset(xt_sc_tab[:].bitcast(I32), 0)
+        z = [sb.tile([P, J if m == TILES - 1 else 2 * J], F32, name=f"z{m}", align_bytes=64) for m in range(TILES)]
+        for m in range(TILES - 1):
+            nc.vector.memset(z[m][:, J:], 0.0)
 
         def load_w(a):
             rows = w[a * K_PASS : (a + 1) * K_PASS, :]
             nc.sync.dma_start(out=w_raw[a][:], in_=rows.rearrange("(p j) n -> p j n", j=PACK))
 
+        def load_xt_scales(first, last):
+            for a, quad in [divmod(piece, 4) for piece in range(first, last)]:
+                row = 32 * quad + XT_PLANE[a]
+                nc.sync.dma_start(
+                    out=xt_sc_tab[row : row + 4, :].bitcast(I32),
+                    in_=xt_scales[a, 4 * quad : 4 * quad + 4, :].bitcast(I32),
+                )
+
         def load_xt(a):
             nc.sync.dma_start(out=xt_tab[a][:], in_=xt_words[a].rearrange("p c r -> p (c r)").bitcast(I32))
 
-        load_w(0)
+        nc.sync.dma_start(out=wi_raw[:], in_=wi_words[0].rearrange("p c r -> p (c r)").bitcast(I32))
         nc.sync.dma_start(slot_list[:], offs)
-        for quad in range(4):
-            nc.gpsimd.dma_start(
-                out=xt_sc_tab[32 * quad : 32 * quad + 4 * PASSES, :].bitcast(I32),
-                in_=xt_scales[:, 4 * quad : 4 * quad + 4, :].bitcast(I32),
-            )
+        nc.sync.dma_start(out=xi_codes[:].bitcast(I32), in_=xi_words[0].bitcast(I32))
         for quad in range(4):
             nc.sync.dma_start(
                 out=xi_sc[32 * quad : 32 * quad + 4, :].bitcast(I32),
                 in_=xi_scales[0, 4 * quad : 4 * quad + 4, :].bitcast(I32),
             )
-        nc.sync.dma_start(head_lists[:], offs2)
-        load_xt(0)
+        load_w(0)
         for quad in range(4):
             nc.sync.dma_start(
                 out=wi_sc_raw[32 * quad : 32 * quad + 4, :].bitcast(I32),
                 in_=wi_scales[0, 4 * quad : 4 * quad + 4, :].bitcast(I32),
             )
-        nc.sync.dma_start(out=wi_raw[:], in_=wi_words[0].rearrange("p c r -> p (c r)").bitcast(I32))
-        nc.sync.dma_start(out=xi_codes[:].bitcast(I32), in_=xi_words[0].bitcast(I32))
+        load_xt_scales(0, 2)
+        load_xt(0)
+        load_xt_scales(2, 8)
         load_w(1)
+        nc.sync.dma_start(head_lists[:], offs2)
         load_xt(1)
 
         wi_codes = sb.tile([P, TILES, P], U32, name="wi_codes", align_bytes=64)
         wi_sc = sb.tile([P, TILES, P], U8, name="wi_sc", align_bytes=64)
+        xt_sc = sb.tile([P, J], U8, name="xt_sc", align_bytes=64)
 
         w_codes = [sb.tile([P, N], U32, name=f"w_codes{a}", align_bytes=64) for a in range(PASSES)]
         w_sc = [sb.tile([P, N], U8, name=f"w_sc{a}", align_bytes=64) for a in range(PASSES)]
@@ -110,13 +120,11 @@ def tile_list_shared_list_then_heads_kernel(
                 lhsT=w_codes[a][:, cols].bitcast(FP8X4),
                 lhsT_scale=w_sc[a][:, cols],
                 rhs=xt_codes[a][:, lo:hi].bitcast(FP8X4),
-                rhs_scale=xt_sc[4 * a :, lo:hi],
+                rhs_scale=xt_sc[XT_PLANE[a] :, lo:hi],
                 start=(a == 0),
                 stop=(a == PASSES - 1),
             )
 
-        quantise_w(0)
-        gather_xt(0, 0, J)
         nc.vector.tensor_copy(
             out=wi_codes[:].rearrange("p m (s u) -> p m s u", u=RUN),
             in_=wi_raw[:].bitcast(U32).rearrange("p (s m u) -> p m s u", m=TILES, u=RUN),
@@ -125,7 +133,8 @@ def tile_list_shared_list_then_heads_kernel(
             out=wi_sc[:].bitcast(I32).rearrange("p m s -> p s m"),
             in_=wi_sc_raw[:].bitcast(I32).rearrange("p (s m) -> p s m", m=TILES),
         )
-        xt_sc = sb.tile([P, J], U8, name="xt_sc", tag="wi_then_xt_sc", align_bytes=64)
+        quantise_w(0)
+        gather_xt(0, 0, J)
         nc.vector.tensor_copy(xt_sc[:], xt_sc_tab[:].indirect(slot_list[:]))
 
         q = [sb.tile([P, I], F32, name=f"q{m}", align_bytes=64) for m in range(TILES)]
@@ -142,7 +151,7 @@ def tile_list_shared_list_then_heads_kernel(
             )
             nc.scalar.copy(out=q[m][:], in_=q_acc[:])
 
-        pieces = [(0, 0, HALF), (0, HALF, J)] + [(m, 0, J) for m in range(1, TILES)]
+        pieces = [(0, 0, HALF), (0, HALF, HALF + P), (0, HALF + P, J)] + [(m, 0, J) for m in range(1, TILES)]
         z_acc = [psum.tile([P, hi - lo], F32, name=f"z_acc{m}_{lo}") for m, lo, hi in pieces]
         for acc, (m, lo, hi) in zip(z_acc, pieces):
             z_pass(acc[:], 0, m, lo, hi)
@@ -151,21 +160,19 @@ def tile_list_shared_list_then_heads_kernel(
         gather_xt(1, 0, HALF)
         gather_xt(1, HALF, J)
 
-        z = [sb.tile([P, J], F32, name=f"z{m}", align_bytes=64) for m in range(TILES)]
         for acc, (m, lo, hi) in zip(z_acc, pieces):
             z_pass(acc[:], 1, m, lo, hi)
-            nc.scalar.copy(out=z[m][:, lo:hi], in_=acc[:])
+            if (m, lo) == (0, HALF):
+                nc.vector.tensor_copy(out=z[m][:, lo:hi], in_=acc[:])
+            else:
+                nc.scalar.copy(out=z[m][:, lo:hi], in_=acc[:])
 
         out_rows = out.rearrange("(s m u) i -> m s u i", m=TILES, u=RUN)
         for m in range(TILES):
             y = sb.tile([P, I], F32, name=f"y{m}", align_bytes=64)
             last = m == TILES - 1
-            cut = 384 if last else I // 2
-            for lo, hi in ((0, cut), (cut, I)):
+            for lo, hi in ((0, 384), (384, I)) if last else ((0, I),):
                 nc.vector.tensor_tensor(
                     y[:, lo:hi], z[m][:].indirect(head_lists[:, lo // 16 : hi // 16]), q[m][:, lo:hi], MULT
                 )
-                if last:
-                    nc.sync.dma_start(out=out_rows[m, :, :, lo:hi], in_=y[:, lo:hi])
-            if not last:
-                nc.sync.dma_start(out=out_rows[m], in_=y[:])
+                nc.sync.dma_start(out=out_rows[m, :, :, lo:hi], in_=y[:, lo:hi])

from contextlib import ExitStack

import concourse.mybir as mybir

K, T, J, I, L, N = 1024, 2048, 512, 512, 512, 512
FLOPS = 2 * K * N * J + 2 * L * N * I

F32 = mybir.dt.float32
BF16 = mybir.dt.bfloat16
I32 = mybir.dt.int32
U32 = mybir.dt.uint32
U16 = mybir.dt.uint16
U8 = mybir.dt.uint8
FP8X4 = mybir.dt.float8_e4m3fn_x4
FP4X4 = mybir.dt.float4_e2m1fn_x4
MULT = mybir.AluOpType.mult

P = 128
PACK = 4
K_PASS = P * PACK
PASSES = K // K_PASS
TILES = N // P
HALF = J // 2
VECTOR_TILES = 3
RUN = 4
XT_PLANE = (8, 12)


def tile_list_shared_list_then_heads_kernel(
    tc, xt_words, xt_scales, w, xi_words, xi_scales, wi_words, wi_scales, offs, offs2, out
):
    nc = tc.nc
    with ExitStack() as ctx:
        sb = ctx.enter_context(tc.tile_pool(name="sb", bufs=1))
        psum = ctx.enter_context(tc.psum_pool(name="psum", bufs=1))
        psq = ctx.enter_context(tc.psum_pool(name="psq", bufs=2))

        slot_list = sb.tile([P, J // 16], U16, name="slot_list")
        head_lists = sb.tile([P, I // 16], U16, name="head_lists")
        xt_tab = [sb.tile([P, T], I32, name=f"xt_tab{a}", align_bytes=64) for a in range(PASSES)]
        xt_sc_tab = sb.tile([P, T], U8, name="xt_sc_tab", align_bytes=64)
        w_raw = [sb.tile([P, PACK, N], F32, name=f"w_raw{a}", align_bytes=64) for a in range(PASSES)]
        wi_raw = sb.tile([P, N], I32, name="wi_raw", align_bytes=64)
        wi_sc_raw = sb.tile([P, N], U8, name="wi_sc_raw", align_bytes=64)
        xi_codes = sb.tile([P, 2 * I], U8, name="xi_codes", align_bytes=64)
        xi_sc = sb.tile([P, I], U8, name="xi_sc", align_bytes=64)

        nc.vector.memset(wi_sc_raw[:].bitcast(I32), 0)
        nc.vector.memset(xt_sc_tab[:].bitcast(I32), 0)
        z = [sb.tile([P, J if m == TILES - 1 else 2 * J], F32, name=f"z{m}", align_bytes=64) for m in range(TILES)]
        for m in range(TILES - 1):
            nc.vector.memset(z[m][:, J:], 0.0)

        def load_w(a):
            rows = w[a * K_PASS : (a + 1) * K_PASS, :]
            nc.sync.dma_start(out=w_raw[a][:], in_=rows.rearrange("(p j) n -> p j n", j=PACK))

        def load_xt_scales(first, last):
            for a, quad in [divmod(piece, 4) for piece in range(first, last)]:
                row = 32 * quad + XT_PLANE[a]
                nc.sync.dma_start(
                    out=xt_sc_tab[row : row + 4, :].bitcast(I32),
                    in_=xt_scales[a, 4 * quad : 4 * quad + 4, :].bitcast(I32),
                )

        def load_xt(a):
            nc.sync.dma_start(out=xt_tab[a][:], in_=xt_words[a].rearrange("p c r -> p (c r)").bitcast(I32))

        nc.sync.dma_start(out=wi_raw[:], in_=wi_words[0].rearrange("p c r -> p (c r)").bitcast(I32))
        nc.sync.dma_start(slot_list[:], offs)
        nc.sync.dma_start(out=xi_codes[:].bitcast(I32), in_=xi_words[0].bitcast(I32))
        for quad in range(4):
            nc.sync.dma_start(
                out=xi_sc[32 * quad : 32 * quad + 4, :].bitcast(I32),
                in_=xi_scales[0, 4 * quad : 4 * quad + 4, :].bitcast(I32),
            )
        load_w(0)
        for quad in range(4):
            nc.sync.dma_start(
                out=wi_sc_raw[32 * quad : 32 * quad + 4, :].bitcast(I32),
                in_=wi_scales[0, 4 * quad : 4 * quad + 4, :].bitcast(I32),
            )
        load_xt_scales(0, 2)
        load_xt(0)
        load_xt_scales(2, 8)
        load_w(1)
        nc.sync.dma_start(head_lists[:], offs2)
        load_xt(1)

        wi_codes = sb.tile([P, TILES, P], U32, name="wi_codes", align_bytes=64)
        wi_sc = sb.tile([P, TILES, P], U8, name="wi_sc", align_bytes=64)
        xt_sc = sb.tile([P, J], U8, name="xt_sc", align_bytes=64)

        w_codes = [sb.tile([P, N], U32, name=f"w_codes{a}", align_bytes=64) for a in range(PASSES)]
        w_sc = [sb.tile([P, N], U8, name=f"w_sc{a}", align_bytes=64) for a in range(PASSES)]
        grouped = [sb.tile([P, TILES, P, PACK], BF16, name=f"grouped{a}", align_bytes=64) for a in range(PASSES)]

        def quantise_w(a):
            src = w_raw[a][:].rearrange("p j (s m u) -> p s m j u", m=TILES, u=RUN)
            dst = grouped[a][:].rearrange("p m (s u) j -> p s m j u", u=RUN)
            nc.vector.tensor_copy(out=dst[:, :, :VECTOR_TILES], in_=src[:, :, :VECTOR_TILES])
            nc.scalar.copy(out=dst[:, :, VECTOR_TILES:], in_=src[:, :, VECTOR_TILES:])
            nc.vector.quantize_mx(
                out=w_codes[a][:].bitcast(FP8X4),
                scales=w_sc[a][:],
                in_=grouped[a][:].rearrange("p m q j -> p (m q j)"),
            )

        xt_codes = [sb.tile([P, J], U32, name=f"xt_codes{a}", align_bytes=64) for a in range(PASSES)]

        def gather_xt(a, lo, hi):
            nc.vector.tensor_copy(
                xt_codes[a][:, lo:hi], xt_tab[a][:].bitcast(U32).indirect(slot_list[:, lo // 16 : hi // 16])
            )

        def z_pass(acc, a, m, lo, hi):
            cols = slice(m * P, (m + 1) * P)
            nc.tensor.matmul_mx(
                out=acc,
                lhsT=w_codes[a][:, cols].bitcast(FP8X4),
                lhsT_scale=w_sc[a][:, cols],
                rhs=xt_codes[a][:, lo:hi].bitcast(FP8X4),
                rhs_scale=xt_sc[XT_PLANE[a] :, lo:hi],
                start=(a == 0),
                stop=(a == PASSES - 1),
            )

        nc.vector.tensor_copy(
            out=wi_codes[:].rearrange("p m (s u) -> p m s u", u=RUN),
            in_=wi_raw[:].bitcast(U32).rearrange("p (s m u) -> p m s u", m=TILES, u=RUN),
        )
        nc.vector.tensor_copy(
            out=wi_sc[:].bitcast(I32).rearrange("p m s -> p s m"),
            in_=wi_sc_raw[:].bitcast(I32).rearrange("p (s m) -> p s m", m=TILES),
        )
        quantise_w(0)
        gather_xt(0, 0, J)
        nc.vector.tensor_copy(xt_sc[:], xt_sc_tab[:].indirect(slot_list[:]))

        q = [sb.tile([P, I], F32, name=f"q{m}", align_bytes=64) for m in range(TILES)]
        for m in range(TILES):
            q_acc = psq.tile([P, I], F32, name="q_acc")
            nc.tensor.matmul_mx(
                out=q_acc[:],
                lhsT=wi_codes[:, m, :].bitcast(FP8X4),
                lhsT_scale=wi_sc[:, m, :],
                rhs=xi_codes[:].bitcast(FP4X4),
                rhs_scale=xi_sc[:],
                start=True,
                stop=True,
            )
            nc.scalar.copy(out=q[m][:], in_=q_acc[:])

        pieces = [(0, 0, HALF), (0, HALF, HALF + P), (0, HALF + P, J)] + [(m, 0, J) for m in range(1, TILES)]
        z_acc = [psum.tile([P, hi - lo], F32, name=f"z_acc{m}_{lo}") for m, lo, hi in pieces]
        for acc, (m, lo, hi) in zip(z_acc, pieces):
            z_pass(acc[:], 0, m, lo, hi)

        quantise_w(1)
        gather_xt(1, 0, HALF)
        gather_xt(1, HALF, J)

        for acc, (m, lo, hi) in zip(z_acc, pieces):
            z_pass(acc[:], 1, m, lo, hi)
            if (m, lo) == (0, HALF):
                nc.vector.tensor_copy(out=z[m][:, lo:hi], in_=acc[:])
            else:
                nc.scalar.copy(out=z[m][:, lo:hi], in_=acc[:])

        out_rows = out.rearrange("(s m u) i -> m s u i", m=TILES, u=RUN)
        for m in range(TILES):
            y = sb.tile([P, I], F32, name=f"y{m}", align_bytes=64)
            last = m == TILES - 1
            for lo, hi in ((0, 384), (384, I)) if last else ((0, I),):
                nc.vector.tensor_tensor(
                    y[:, lo:hi], z[m][:].indirect(head_lists[:, lo // 16 : hi // 16]), q[m][:, lo:hi], MULT
                )
                nc.sync.dma_start(out=out_rows[m, :, :, lo:hi], in_=y[:, lo:hi])
